import numpy as np
import ml_dtypes


def mxq(x, axis, fmt="e4m3"):
    dtype, down = {"e4m3": (ml_dtypes.float8_e4m3fn, 7), "e5m2": (ml_dtypes.float8_e5m2, 14)}[fmt]
    v = np.moveaxis(np.asarray(x, np.float32).astype(ml_dtypes.bfloat16).astype(np.float64), axis, -1)
    blocks = v.reshape(v.shape[:-1] + (-1, 32))
    amax = np.abs(blocks).max(-1, keepdims=True)
    byte = np.maximum(np.where(amax > 0, np.frexp(amax)[1] - 1 + 127, 0) - down, 1)
    scale = np.exp2(byte - 127.0)
    codes = (blocks / scale).astype(np.float32).astype(dtype).astype(np.float64)
    return np.moveaxis((codes * scale).reshape(v.shape), -1, axis)


WIDE = False


def mx_kscale(k):
    if not WIDE:
        return np.ones(k)
    levels = np.array([10, -10, 5, -5, 0])
    if k % 512:
        return np.exp2(np.random.permutation(np.resize(levels, k // 32))).repeat(32)
    a = np.empty((k // 512, 16))
    for p in range(k // 512):
        a[p, :8] = np.random.permutation(np.resize(levels, 8))
        for g in range(8):
            far = levels[np.abs(levels - a[p, g]) >= 10]
            a[p, g + 8] = far[np.random.randint(len(far))]
    return np.exp2(a.ravel()).repeat(32)


BF16 = ml_dtypes.bfloat16


def bf(x):
    return np.asarray(x, np.float32).astype(BF16)


def f64(x):
    return np.asarray(x).astype(np.float64)


E2M1 = np.array([0.0, 0.5, 1.0, 1.5, 2.0, 3.0, 4.0, 6.0, -0.0, -0.5, -1.0, -1.5, -2.0, -3.0, -4.0, -6.0])


def pack_weight(w, fmt):
    k, n = w.shape
    w = f64(bf(w)).reshape(k // 32, 32, n)
    amax = np.abs(w).max(1)
    if fmt == "e4m3":
        byte = np.frexp(amax)[1] - 1 + 127 - 7
    else:
        mant, ex = np.frexp(amax / 6.0)
        byte = np.where(mant > 0.5, ex, ex - 1) + 127
    byte = np.clip(np.where(amax > 0, byte, 1), 1, 254)
    scaled = (w * np.exp2(127.0 - byte)[:, None, :]).reshape(k, n).astype(np.float32)
    by_word = np.ascontiguousarray(scaled.reshape(k // 512, 128, 4, n).transpose(0, 1, 3, 2))
    if fmt == "e4m3":
        words = by_word.astype(ml_dtypes.float8_e4m3fn).view(np.uint8)
    else:
        c = by_word.astype(ml_dtypes.float4_e2m1fn).view(np.uint8) & 0xF
        words = c[..., 0::2] | (c[..., 1::2] << 4)
    return np.ascontiguousarray(words), np.ascontiguousarray(byte.astype(np.uint8).reshape(k // 512, 16, n))


def unpack_weight(words, scales, fmt):
    g, p, n, _ = words.shape
    if fmt == "e4m3":
        vals = np.ascontiguousarray(words).view(ml_dtypes.float8_e4m3fn).astype(np.float64)
    else:
        nib = np.empty((g, p, n, 4), np.uint8)
        nib[..., 0::2] = words & 0xF
        nib[..., 1::2] = words >> 4
        vals = E2M1[nib]
    vals = vals * np.repeat(np.exp2(scales.astype(np.float64) - 127.0), 8, axis=1)[..., None]
    return vals.transpose(0, 1, 3, 2).reshape(g * 512, n)
def pack4(w):
    words, scales = pack_weight(w, "e2m1")
    return words.reshape(words.shape[0], 128, -1), scales


def unpack4(words, scales):
    return unpack_weight(words.reshape(words.shape[0], 128, -1, 2), scales, "e2m1")


def planes(Y):
    n, m = Y.shape
    b = f64(bf(Y)).reshape(n // 32, 32, m)
    amax = np.abs(b).max(1)
    byte = np.clip(np.where(amax > 0, np.frexp(amax)[1] - 1 + 127 - 7, 1), 1, 254)
    codes = (b * np.exp2(127.0 - byte)[:, None, :]).reshape(n, m).astype(np.float32).astype(ml_dtypes.float8_e4m3fn).view(np.uint8)
    words = codes.reshape(n // 512, 128, 4, m).transpose(0, 1, 3, 2)
    return np.ascontiguousarray(words), np.ascontiguousarray(byte.astype(np.uint8).reshape(n // 512, 16, m))


T, K, N = 2048, 1024, 1536
PART = 0.5
SHARE = 0.3
DAMP = 0.3

def setup_inputs():
    s = mx_kscale(T)
    t = mx_kscale(K)
    chan = np.exp(0.6 * np.random.randn(K))
    load = SHARE * np.random.randn(K)
    x = (np.random.randn(T, K) + np.random.randn(T, 1) * load) * chan
    w = PART * np.exp(0.5 * np.random.randn(T, 1)) / T
    xw_words, xw_scales = pack4(x * w / s[:, None])
    x_words, x_scales = pack4(x * s[:, None] * t)
    r = np.random.randn(K, K)
    prior = PART * (np.eye(K) + load[:, None] * load + 0.2 * (r + r.T) / np.sqrt(K)) * chan[:, None] * chan
    err = np.random.rand(K, N) - 0.5
    return {"xw_words": xw_words, "xw_scales": xw_scales,
            "x_words": x_words, "x_scales": x_scales,
            "prior": bf(prior * t),
            "err": bf(err / t[:, None]),
            "damp": bf(DAMP * np.exp(0.3 * np.random.randn(K)) * t),
            "step": bf(np.exp(0.5 * np.random.randn(N)))}

def reference(xw_words, xw_scales, x_words, x_scales, prior, err, damp, step):
    xw = unpack4(xw_words, xw_scales)
    x = unpack4(x_words, x_scales)
    h = (xw.T @ x) + f64(prior)
    e = f64(err)
    he = mxq(h, 1) @ mxq(e, 0)
    y = (he + f64(damp)[:, None] * e) * f64(step)
    Y = y.reshape(K, N)
    words, scales = planes(Y)
    return y, words, scales

@@ -1,0 +1,433 @@
+from contextlib import ExitStack
+
+import concourse.mybir as mybir
+from concourse.masks import make_identity
+
+T, K, N = 2048, 1024, 1536
+FLOPS = 2 * T * K * K + 2 * K * K * N
+
+F32 = mybir.dt.float32
+BF16 = mybir.dt.bfloat16
+I32 = mybir.dt.int32
+U32 = mybir.dt.uint32
+U8 = mybir.dt.uint8
+FP8X4 = mybir.dt.float8_e4m3fn_x4
+FP4X4 = mybir.dt.float4_e2m1fn_x4
+ADD = mybir.AluOpType.add
+MULT = mybir.AluOpType.mult
+
+P = 128
+W = 512
+
+
+def tile_gptq_damped_gram_error_k5_kernel(
+    tc, xw_words, xw_scales, x_words, x_scales, prior, err, damp, step, out_0, out_1, out_2
+):
+    nc = tc.nc
+    with ExitStack() as ctx:
+        sb = ctx.enter_context(tc.tile_pool(name="sb", bufs=1))
+        ps = ctx.enter_context(tc.psum_pool(name="ps", bufs=1))
+        ctx.enter_context(tc.manual_schedule())
+
+        def keep(name, shape, dtype):
+            return sb.tile(shape, dtype, name=name, align_bytes=64)
+
+        free_banks = list(range(6))
+        held = {}
+
+        def take_bank(key):
+            b = free_banks.pop(0)
+            bank = ps.tile([P, W], F32, name="bank%d" % b, tag="bank%d" % b)
+            held[key] = (b, bank)
+            return bank
+
+        def give_bank(key):
+            b, bank = held.pop(key)
+            free_banks.append(b)
+            return bank
+
+        words = {}
+        planes = {(op, half): keep("planes%d_%d" % (op, half), [P, 4, W], U8) for op in range(2) for half in range(2)}
+        src_words = [xw_words.bitcast(I32), x_words.bitcast(I32)]
+        src_scales = [xw_scales.bitcast(I32), x_scales.bitcast(I32)]
+        XW, X = 0, 1
+
+        def load_words(op, half, g0, g1):
+            t = keep("words%d_%d_%d" % (op, half, g0), [P, g1 - g0, 2 * W], U8)
+            nc.sync.dma_start(
+                out=t[:].bitcast(I32),
+                in_=src_words[op][g0:g1, :, 256 * half : 256 * (half + 1)].rearrange("g p w -> p g w"),
+            )
+            for g in range(g0, g1):
+                words[(op, half, g)] = t[:, g - g0, :]
+
+        def load_scales(op, half):
+            for r in range(4):
+                nc.sync.dma_start(
+                    out=planes[(op, half)][r:P:32, :, :].bitcast(I32),
+                    in_=src_scales[op][:, r:16:4, 128 * half : 128 * (half + 1)].rearrange("g q w -> q g w"),
+                )
+
+        e_raw = {}
+
+        def load_err(h, c):
+            t = keep("e_raw%d_%d" % (h, c), [P, 4, W], BF16)
+            nc.sync.dma_start(
+                out=t[:], in_=err[W * h : W * (h + 1), W * c : W * (c + 1)].rearrange("(p t) n -> p t n", t=4)
+            )
+            e_raw[(h, c)] = t
+
+        p_raw = {}
+
+        def load_prior(g, h, a0, a1):
+            t = keep("p_raw%d_%d_%d" % (g, h, a0), [P, a1 - a0, W], BF16)
+            nc.sync.dma_start(
+                out=t[:],
+                in_=prior[W * g + P * a0 : W * g + P * a1, W * h : W * (h + 1)].rearrange("(a r) j -> r a j", r=P),
+            )
+            for a in range(a0, a1):
+                p_raw[(g, h, a)] = t[:, a - a0, :]
+
+        def copy_on(engine, out, in_):
+            if engine == "S":
+                nc.scalar.copy(out=out, in_=in_)
+            else:
+                nc.vector.tensor_copy(out=out, in_=in_)
+
+        def side_by_side(engine, out, in_):
+            copy_on(engine, out.rearrange("p (c i) t -> p c t i", i=4), in_.rearrange("p t (c i) -> p c t i", i=4))
+
+        def gram_pass(g, h, a, tg):
+            if tg == 0:
+                take_bank(("gram", g, h, a))
+            bank = held[("gram", g, h, a)][1]
+            nc.tensor.matmul_mx(
+                out=bank[:],
+                lhsT=words[(XW, g, tg)][:, 256 * a : 256 * (a + 1)].bitcast(FP4X4),
+                lhsT_scale=planes[(XW, g)][:, tg, P * a : P * (a + 1)],
+                rhs=words[(X, h, tg)].bitcast(FP4X4),
+                rhs_scale=planes[(X, h)][:, tg, :],
+                start=(tg == 0),
+                stop=(tg == 3),
+            )
+
+        def gram(g, h, a):
+            for tg in range(4):
+                gram_pass(g, h, a, tg)
+
+        h_rows = {}
+
+        def add_prior(g, h, a):
+            bank = give_bank(("gram", g, h, a))
+            t = keep("h_rows%d_%d_%d" % (g, h, a), [P, W], BF16)
+            nc.vector.tensor_tensor(
+                out=t[:].rearrange("q (u p e) -> q u p e", u=2, e=2),
+                in0=bank[:].rearrange("q (p u e) -> q u p e", u=2, e=2),
+                in1=p_raw[(g, h, a)].rearrange("q (p u e) -> q u p e", u=2, e=2),
+                op=ADD,
+            )
+            h_rows[(g, h, a)] = t
+
+        def turn(g, h, pair):
+            bank = take_bank(("turn", g, h, pair))
+            for a2 in range(2):
+                pairs = h_rows[(g, h, 2 * pair + a2)][:].bitcast(F32)
+                for u in range(2):
+                    at = 256 * u + P * a2
+                    nc.tensor.transpose(bank[:, at : at + P], pairs[:, P * u : P * (u + 1)], ident[:])
+
+        h_cols = {(g, h): keep("h_cols%d_%d" % (g, h), [P, 4 * W], BF16) for g in range(2) for h in range(2)}
+        h_codes = {(g, h): keep("h_codes%d_%d" % (g, h), [P, W], U32) for g in range(2) for h in range(2)}
+        h_scales = {(g, h): keep("h_scales%d_%d" % (g, h), [P, W], U8) for g in range(2) for h in range(2)}
+
+        def spill(engine, g, h, pair):
+            bank = give_bank(("turn", g, h, pair))
+            dst = h_cols[(g, h)][:].bitcast(F32).rearrange("q (t m u) -> q t m u", t=4, u=2)
+            copy_on(engine, dst[:, :, 64 * pair : 64 * (pair + 1), :], bank[:].rearrange("q (u m t) -> q t m u", u=2, t=4))
+
+        def quant_h(g, h, t0, t1):
+            nc.vector.quantize_mx(
+                out=h_codes[(g, h)][:, P * t0 : P * t1].bitcast(FP8X4),
+                scales=h_scales[(g, h)][:, P * t0 : P * t1],
+                in_=h_cols[(g, h)][:, W * t0 : W * t1],
+            )
+
+        e_side = [keep("e_side%d" % c, [P, 2, W, 4], BF16) for c in range(3)]
+        e_codes = [keep("e_codes%d" % c, [P, 2, W], U32) for c in range(3)]
+        e_scales = [keep("e_scales%d" % c, [P, 2, W], U8) for c in range(3)]
+
+        def lay_err(engine, h, c, lo=0, hi=W):
+            side_by_side(engine, e_side[c][:, h, lo:hi, :], e_raw[(h, c)][:, :, lo:hi])
+
+        def quant_err(c, h0, h1):
+            nc.vector.quantize_mx(
+                out=e_codes[c][:, h0:h1, :].rearrange("p h n -> p (h n)").bitcast(FP8X4),
+                scales=e_scales[c][:, h0:h1, :].rearrange("p h n -> p (h n)"),
+                in_=e_side[c][:, h0:h1, :, :].rearrange("p h n t -> p (h n t)"),
+            )
+
+        def product_pass(u, t, h):
+            g, n0, w = u
+            c, o = divmod(n0, W)
+            if h == 0:
+                take_bank(("prod", u, t))
+            bank = held[("prod", u, t)][1]
+            nc.tensor.matmul_mx(
+                out=bank[:, :w],
+                lhsT=h_codes[(g, h)][:, P * t : P * (t + 1)].bitcast(FP8X4),
+                lhsT_scale=h_scales[(g, h)][:, P * t : P * (t + 1)],
+                rhs=e_codes[c][:, h, o : o + w].bitcast(FP8X4),
+                rhs_scale=e_scales[c][:, h, o : o + w],
+                start=(h == 0),
+                stop=(h == 1),
+            )
+
+        def product(u, ts):
+            for t in ts:
+                for h in range(2):
+                    product_pass(u, t, h)
+
+        damped, y32, y16 = {}, {}, {}
+
+        def add_damping(u, t):
+            g, n0, w = u
+            c, o = divmod(n0, W)
+            if t == 0:
+                damped[u] = sb.tile([P, 4, w], F32, name="damped", tag="damped", bufs=3)
+                y32[u] = sb.tile([P, 4, w], F32, name="y32", tag="y32", bufs=4)
+            bank = give_bank(("prod", u, t))
+            nc.vector.scalar_tensor_tensor(
+                out=damped[u][:, t, :], in0=e_raw[(g, c)][:, t, o : o + w], scalar=damp_sb[:, g, t : t + 1],
+                in1=bank[:, :w], op0=MULT, op1=ADD,
+            )
+
+        def pool_step(u, t, lo, hi):
+            g, n0, w = u
+            nc.gpsimd.tensor_tensor(
+                out=y32[u][:, t, lo:hi], in0=damped[u][:, t, lo:hi], in1=step_all[:, n0 + lo : n0 + hi], op=MULT
+            )
+
+        def vector_step(u, t, lo, hi):
+            g, n0, w = u
+            c, o = divmod(n0, W)
+            nc.vector.tensor_tensor(
+                out=y32[u][:, t, lo:hi].rearrange("q (p b e) -> q p b e", b=2, e=2),
+                in0=damped[u][:, t, lo:hi].rearrange("q (p b e) -> q p b e", b=2, e=2),
+                in1=step_psum[c][:, (o + lo) // 4 : (o + hi) // 4, :, :],
+                op=MULT,
+            )
+
+        def store_y(u, t0, t1):
+            g, n0, w = u
+            nc.sync.dma_start(
+                out=out_0[W * g : W * (g + 1), n0 : n0 + w].rearrange("(p t) n -> p t n", t=4)[:, t0:t1, :],
+                in_=y32[u][:, t0:t1, :],
+            )
+
+        def round_y(engine, u, lo, hi):
+            if u not in y16:
+                y16[u] = sb.tile([P, u[2], 4], BF16, name="y16", tag="y16", bufs=3, align_bytes=64)
+            side_by_side(engine, y16[u][:, lo:hi, :], y32[u][:, :, lo:hi])
+
+        y_codes = [keep("y_codes%d" % g, [P, N], U32) for g in range(2)]
+        y_scales = [keep("y_scales%d" % g, [P, N], U8) for g in range(2)]
+        dst_words = out_1.rearrange("g p m t -> g p (m t)").bitcast(I32)
+        dst_scales = out_2.bitcast(I32)
+
+        def quant_y(u):
+            g, n0, w = u
+            nc.vector.quantize_mx(
+                out=y_codes[g][:, n0 : n0 + w].bitcast(FP8X4),
+                scales=y_scales[g][:, n0 : n0 + w],
+                in_=y16[u][:].rearrange("p n t -> p (n t)"),
+            )
+            nc.sync.dma_start(out=dst_words[g, :, n0 : n0 + w], in_=y_codes[g][:, n0 : n0 + w].bitcast(I32))
+
+        def store_scales(g, lo, hi, queues):
+            for r in range(4):
+                queues[r].dma_start(
+                    out=dst_scales[g, r:16:4, lo // 4 : hi // 4], in_=y_scales[g][r:P:32, lo:hi].bitcast(I32)
+                )
+
+        step_cols = keep("step_cols", [P, 3, 4], BF16)
+        damp_sb = keep("damp_sb", [P, 2, 4], BF16)
+        ident = keep("ident", [P, P], F32)
+        step_all = keep("step_all", [P, N], F32)
+
+        nc.gpsimd.dma_start(out=step_cols[:], in_=step.rearrange("(c p b) -> p c b", c=3, b=4))
+        for half in range(2):
+            for op in (X, XW):
+                nc.vector.memset(planes[(op, half)][:].rearrange("p g w -> p (g w)").bitcast(I32), 0)
+        make_identity(nc, ident[:])
+        nc.gpsimd.dma_start(out=damp_sb[:], in_=damp.rearrange("(g p t) -> p g t", g=2, t=4))
+        load_words(X, 0, 0, 1)
+        load_words(XW, 0, 0, 1)
+        load_scales(X, 0)
+        load_scales(XW, 0)
+        load_words(X, 0, 1, 2)
+        load_words(XW, 0, 1, 2)
+        load_words(X, 0, 2, 4)
+        load_words(XW, 0, 2, 4)
+        load_err(0, 0)
+        load_scales(X, 1)
+        load_words(X, 1, 0, 4)
+        load_prior(0, 0, 0, 4)
+        load_err(1, 0)
+        load_prior(0, 1, 0, 2)
+        load_prior(0, 1, 2, 4)
+        load_scales(XW, 1)
+        load_words(XW, 1, 0, 4)
+        load_err(0, 1)
+        load_err(1, 1)
+        load_prior(1, 0, 0, 4)
+        load_err(0, 2)
+        load_err(1, 2)
+        load_prior(1, 1, 0, 4)
+
+        step_pairs = step_cols[:].bitcast(F32)
+        step_banks = [ps.tile([P, W], F32, name="step_bank%d" % i, tag="step_bank%d" % i) for i in range(2)]
+        step_psum = []
+        for c in range(3):
+            half_bank = step_banks[c // 2][:, 256 * (c % 2) : 256 * (c % 2 + 1)]
+            for b in range(2):
+                nc.tensor.transpose(
+                    half_bank[:, P * b : P * (b + 1)], step_pairs[:, c, b : b + 1].to_broadcast([P, P]), ident[:]
+                )
+            step_psum.append(half_bank.bitcast(BF16).rearrange("q (b p e) -> q p b e", b=2, e=2))
+        for c in range(3):
+            nc.scalar.copy(
+                out=step_all[:, W * c : W * (c + 1)].rearrange("q (p b e) -> q p b e", b=2, e=2), in_=step_psum[c]
+            )
+
+        for tg in range(4):
+            for a in range(4):
+                gram_pass(0, 0, a, tg)
+        lay_err("V", 0, 0)
+        quant_err(0, 0, 1)
+        lay_err("S", 1, 0)
+        gram(0, 1, 0)
+        gram(0, 1, 1)
+        for a in range(4):
+            add_prior(0, 0, a)
+        gram(0, 1, 2)
+        gram(0, 1, 3)
+        add_prior(0, 1, 0)
+        add_prior(0, 1, 1)
+        turn(0, 0, 0)
+        turn(0, 0, 1)
+        turn(0, 1, 0)
+        add_prior(0, 1, 2)
+        add_prior(0, 1, 3)
+        turn(0, 1, 1)
+        spill("S", 0, 0, 0)
+        spill("S", 0, 0, 1)
+        spill("S", 0, 1, 0)
+        spill("S", 0, 1, 1)
+        gram(1, 0, 0)
+        gram(1, 0, 1)
+        quant_err(0, 1, 2)
+        quant_h(0, 0, 0, 4)
+        quant_h(0, 1, 0, 2)
+        quant_h(0, 1, 2, 4)
+        lay_err("S", 0, 1)
+        lay_err("S", 1, 1)
+        u = [(0, 0, W), (0, W, W), (0, 2 * W, W), (1, 0, W), (1, W, W), (1, 2 * W, 256), (1, 2 * W + 256, 128), (1, 2 * W + 384, 128)]
+
+        product(u[0], range(4))
+        add_damping(u[0], 0)
+        pool_step(u[0], 0, 0, W)
+        add_damping(u[0], 1)
+        pool_step(u[0], 1, 0, W)
+        add_damping(u[0], 2)
+        pool_step(u[0], 2, 0, 256)
+        add_damping(u[0], 3)
+        gram(1, 0, 2)
+        gram(1, 0, 3)
+        add_prior(1, 0, 0)
+        vector_step(u[0], 3, 0, W)
+        vector_step(u[0], 2, 256, W)
+        add_prior(1, 0, 1)
+        store_y(u[0], 0, 2)
+        store_y(u[0], 2, 4)
+        quant_err(1, 0, 2)
+        lay_err("S", 0, 2)
+        round_y("S", u[0], 0, W)
+        lay_err("S", 1, 2)
+        product(u[1], range(4))
+        add_prior(1, 0, 2)
+        add_prior(1, 0, 3)
+        add_damping(u[1], 0)
+        pool_step(u[1], 0, 0, W)
+        gram(1, 1, 0)
+        add_damping(u[1], 1)
+        pool_step(u[1], 1, 0, W)
+        turn(1, 0, 0)
+        add_damping(u[1], 2)
+        pool_step(u[1], 2, 0, 256)
+        turn(1, 0, 1)
+        add_damping(u[1], 3)
+        spill("S", 1, 0, 0)
+        spill("S", 1, 0, 1)
+        gram(1, 1, 1)
+        vector_step(u[1], 2, 256, W)
+        vector_step(u[1], 3, 0, W)
+        store_y(u[1], 0, 2)
+        store_y(u[1], 2, 4)
+        round_y("S", u[1], 0, W)
+        add_prior(1, 1, 0)
+        quant_err(2, 0, 2)
+        quant_y(u[0])
+        gram(1, 1, 2)
+        product(u[2], [0, 1])
+        gram(1, 1, 3)
+        add_prior(1, 1, 1)
+        add_prior(1, 1, 2)
+        product(u[2], [2, 3])
+        add_damping(u[2], 0)
+        quant_h(1, 0, 0, 4)
+        pool_step(u[2], 0, 0, W)
+        add_prior(1, 1, 3)
+        turn(1, 1, 0)
+        add_damping(u[2], 1)
+        pool_step(u[2], 1, 0, W)
+        turn(1, 1, 1)
+        spill("S", 1, 1, 0)
+        spill("S", 1, 1, 1)
+        add_damping(u[2], 2)
+        add_damping(u[2], 3)
+        for t in range(4):
+            product_pass(u[3], t, 0)
+        vector_step(u[2], 2, 0, W)
+        quant_h(1, 1, 0, 4)
+        for t in range(4):
+            product_pass(u[3], t, 1)
+        vector_step(u[2], 3, 0, W)
+        store_y(u[2], 0, 2)
+        store_y(u[2], 2, 4)
+        round_y("S", u[2], 0, W)
+        quant_y(u[1])
+        share = {3: 1024, 4: 1024, 5: 512, 6: 128, 7: 0}
+        for i in range(3, 8):
+            w = u[i][2]
+            for t in range(4):
+                add_damping(u[i], t)
+                if t == 0 and i > 3:
+                    quant_y(u[i - 2])
+                n = min(max(share[i] - t * w, 0), w)
+                if n > 0:
+                    pool_step(u[i], t, 0, n)
+                if i + 1 < 8:
+                    product(u[i + 1], [t])
+            for t in range(4):
+                n = min(max(share[i] - t * w, 0), w)
+                if n < w:
+                    vector_step(u[i], t, n, w)
+            store_y(u[i], 0, 2)
+            store_y(u[i], 2, 4)
+            round_y("S", u[i], 0, w)
+            if i == 4:
+                store_scales(0, 0, N, [nc.sync] * 4)
+        quant_y(u[6])
+        store_scales(1, 0, N - 128, [nc.sync] * 4)
+        quant_y(u[7])
+        store_scales(1, N - 128, N, [nc.scalar, nc.scalar, nc.sync, nc.sync])

@@ -18,6 +18,9 @@ MULT = mybir.AluOpType.mult
 
 P = 128
 W = 512
+XW, X = 0, 1
+WORK_BANKS = 6
+UNITS = [(0, 0, W), (0, W, W), (0, 2 * W, W), (1, 0, W), (1, W, W), (1, 2 * W, 256), (1, 2 * W + 256, 256)]
 
 
 def tile_gptq_damped_gram_error_k5_kernel(
@@ -30,83 +33,70 @@ def tile_gptq_damped_gram_error_k5_kernel(
         ctx.enter_context(tc.manual_schedule())
 
         def keep(name, shape, dtype):
-            return sb.tile(shape, dtype, name=name, align_bytes=64)
+            return sb.tile(shape, dtype, name=name, align_bytes=256)
 
-        free_banks = list(range(6))
+        free_banks = list(range(WORK_BANKS))
         held = {}
 
         def take_bank(key):
             b = free_banks.pop(0)
-            bank = ps.tile([P, W], F32, name="bank%d" % b, tag="bank%d" % b)
-            held[key] = (b, bank)
-            return bank
+            held[key] = (b, ps.tile([P, W], F32, name="bank%d" % b, tag="bank%d" % b))
+
+        def bank_of(key):
+            return held[key][1]
 
         def give_bank(key):
             b, bank = held.pop(key)
             free_banks.append(b)
             return bank
 
-        words = {}
-        planes = {(op, half): keep("planes%d_%d" % (op, half), [P, 4, W], U8) for op in range(2) for half in range(2)}
         src_words = [xw_words.bitcast(I32), x_words.bitcast(I32)]
         src_scales = [xw_scales.bitcast(I32), x_scales.bitcast(I32)]
-        XW, X = 0, 1
+        fp4_words = {}
+        fp4_scales = {
+            (op, half): keep("fp4_scales%d_%d" % (op, half), [P, 4, W], U8) for op in (XW, X) for half in range(2)
+        }
+        e_rows, p_rows = {}, {}
 
-        def load_words(op, half, g0, g1):
-            t = keep("words%d_%d_%d" % (op, half, g0), [P, g1 - g0, 2 * W], U8)
-            nc.sync.dma_start(
-                out=t[:].bitcast(I32),
-                in_=src_words[op][g0:g1, :, 256 * half : 256 * (half + 1)].rearrange("g p w -> p g w"),
-            )
-            for g in range(g0, g1):
-                words[(op, half, g)] = t[:, g - g0, :]
+        def load_words(op, halves, tgs):
+            tile = keep("fp4_words%d_%d_%d" % (op, halves[0], tgs[0]), [P, len(tgs), 2 * W * len(halves)], U8)
+            src = src_words[op][tgs[0] : tgs[-1] + 1, :, 256 * halves[0] : 256 * (halves[-1] + 1)]
+            nc.sync.dma_start(out=tile[:].bitcast(I32), in_=src.rearrange("g p w -> p g w"))
+            for n, tg in enumerate(tgs):
+                for m, half in enumerate(halves):
+                    fp4_words[op, half, tg] = tile[:, n, 2 * W * m : 2 * W * (m + 1)]
 
         def load_scales(op, half):
             for r in range(4):
+                src = src_scales[op][:, r:16:4, P * half : P * (half + 1)]
                 nc.sync.dma_start(
-                    out=planes[(op, half)][r:P:32, :, :].bitcast(I32),
-                    in_=src_scales[op][:, r:16:4, 128 * half : 128 * (half + 1)].rearrange("g q w -> q g w"),
+                    out=fp4_scales[op, half][r:P:32, :, :].bitcast(I32), in_=src.rearrange("g q w -> q g w")
                 )
 
-        e_raw = {}
-
         def load_err(h, c):
-            t = keep("e_raw%d_%d" % (h, c), [P, 4, W], BF16)
-            nc.sync.dma_start(
-                out=t[:], in_=err[W * h : W * (h + 1), W * c : W * (c + 1)].rearrange("(p t) n -> p t n", t=4)
-            )
-            e_raw[(h, c)] = t
+            e_rows[h, c] = keep("e_rows%d_%d" % (h, c), [P, 4, W], BF16)
+            src = err[W * h : W * (h + 1), W * c : W * (c + 1)]
+            nc.sync.dma_start(out=e_rows[h, c][:], in_=src.rearrange("(p t) n -> p t n", t=4))
 
-        p_raw = {}
+        def load_prior(g, tiles):
+            tile = keep("p_rows%d_%d" % (g, tiles[0]), [P, len(tiles), K], BF16)
+            src = prior[W * g + P * tiles[0] : W * g + P * (tiles[-1] + 1), :]
+            nc.sync.dma_start(out=tile[:], in_=src.rearrange("(a r) j -> r a j", r=P))
+            for n, a in enumerate(tiles):
+                p_rows[g, a] = tile[:, n, :]
 
-        def load_prior(g, h, a0, a1):
-            t = keep("p_raw%d_%d_%d" % (g, h, a0), [P, a1 - a0, W], BF16)
-            nc.sync.dma_start(
-                out=t[:],
-                in_=prior[W * g + P * a0 : W * g + P * a1, W * h : W * (h + 1)].rearrange("(a r) j -> r a j", r=P),
-            )
-            for a in range(a0, a1):
-                p_raw[(g, h, a)] = t[:, a - a0, :]
-
-        def copy_on(engine, out, in_):
-            if engine == "S":
-                nc.scalar.copy(out=out, in_=in_)
-            else:
-                nc.vector.tensor_copy(out=out, in_=in_)
-
-        def side_by_side(engine, out, in_):
-            copy_on(engine, out.rearrange("p (c i) t -> p c t i", i=4), in_.rearrange("p t (c i) -> p c t i", i=4))
+        def side_by_side(copy, out, in_):
+            copy(out=out.rearrange("p (c i) t -> p c t i", i=4), in_=in_.rearrange("p t (c i) -> p c t i", i=4))
 
         def gram_pass(g, h, a, tg):
             if tg == 0:
                 take_bank(("gram", g, h, a))
-            bank = held[("gram", g, h, a)][1]
             nc.tensor.matmul_mx(
-                out=bank[:],
-                lhsT=words[(XW, g, tg)][:, 256 * a : 256 * (a + 1)].bitcast(FP4X4),
-                lhsT_scale=planes[(XW, g)][:, tg, P * a : P * (a + 1)],
-                rhs=words[(X, h, tg)].bitcast(FP4X4),
-                rhs_scale=planes[(X, h)][:, tg, :],
+                out=bank_of(("gram", g, h, a))[:],
+                lhsT=fp4_words[XW, g, tg][:, 2 * P * a : 2 * P * (a + 1)].bitcast(FP4X4),
+                lhsT_scale=fp4_scales[XW, g][:, tg, P * a : P * (a + 1)],
+                rhs=fp4_words[X, h, tg].bitcast(FP4X4),
+                rhs_scale=fp4_scales[X, h][:, tg, :],
                 start=(tg == 0),
                 stop=(tg == 3),
             )
@@ -119,45 +109,50 @@ def tile_gptq_damped_gram_error_k5_kernel(
 
         def add_prior(g, h, a):
             bank = give_bank(("gram", g, h, a))
-            t = keep("h_rows%d_%d_%d" % (g, h, a), [P, W], BF16)
+            h_rows[g, h, a] = keep("h_rows%d_%d" % (h, a), [P, W], BF16)
             nc.vector.tensor_tensor(
-                out=t[:].rearrange("q (u p e) -> q u p e", u=2, e=2),
-                in0=bank[:].rearrange("q (p u e) -> q u p e", u=2, e=2),
-                in1=p_raw[(g, h, a)].rearrange("q (p u e) -> q u p e", u=2, e=2),
+                out=h_rows[g, h, a][:].rearrange("r (u p e) -> r u p e", u=2, e=2),
+                in0=bank[:].rearrange("r (p u e) -> r u p e", u=2, e=2),
+                in1=p_rows[g, a][:, W * h : W * (h + 1)].rearrange("r (p u e) -> r u p e", u=2, e=2),
                 op=ADD,
             )
-            h_rows[(g, h, a)] = t
 
         def turn(g, h, pair):
-            bank = take_bank(("turn", g, h, pair))
-            for a2 in range(2):
-                pairs = h_rows[(g, h, 2 * pair + a2)][:].bitcast(F32)
+            take_bank(("turn", g, h, pair))
+            for n in range(2):
+                pairs = h_rows[g, h, 2 * pair + n][:].bitcast(F32)
                 for u in range(2):
-                    at = 256 * u + P * a2
-                    nc.tensor.transpose(bank[:, at : at + P], pairs[:, P * u : P * (u + 1)], ident[:])
+                    at = 2 * P * u + P * n
+                    nc.tensor.transpose(
+                        bank_of(("turn", g, h, pair))[:, at : at + P], pairs[:, P * u : P * (u + 1)], ident[:]
+                    )
 
-        h_cols = {(g, h): keep("h_cols%d_%d" % (g, h), [P, 4 * W], BF16) for g in range(2) for h in range(2)}
-        h_codes = {(g, h): keep("h_codes%d_%d" % (g, h), [P, W], U32) for g in range(2) for h in range(2)}
-        h_scales = {(g, h): keep("h_scales%d_%d" % (g, h), [P, W], U8) for g in range(2) for h in range(2)}
+        halves_of_h = [(g, h) for g in range(2) for h in range(2)]
+        h_cols = {key: keep("h_cols%d_%d" % key, [P, 4 * W], BF16) for key in halves_of_h}
+        h_codes = {key: keep("h_codes%d_%d" % key, [P, W], U32) for key in halves_of_h}
+        h_scales = {key: keep("h_scales%d_%d" % key, [P, W], U8) for key in halves_of_h}
 
-        def spill(engine, g, h, pair):
+        def spill(copy, g, h, pair):
             bank = give_bank(("turn", g, h, pair))
-            dst = h_cols[(g, h)][:].bitcast(F32).rearrange("q (t m u) -> q t m u", t=4, u=2)
-            copy_on(engine, dst[:, :, 64 * pair : 64 * (pair + 1), :], bank[:].rearrange("q (u m t) -> q t m u", u=2, t=4))
+            dst = h_cols[g, h][:].bitcast(F32).rearrange("p (t m u) -> p t m u", t=4, u=2)
+            copy(
+                out=dst[:, :, 64 * pair : 64 * (pair + 1), :],
+                in_=bank[:].rearrange("p (u m t) -> p t m u", u=2, t=4),
+            )
 
         def quant_h(g, h, t0, t1):
             nc.vector.quantize_mx(
-                out=h_codes[(g, h)][:, P * t0 : P * t1].bitcast(FP8X4),
-                scales=h_scales[(g, h)][:, P * t0 : P * t1],
-                in_=h_cols[(g, h)][:, W * t0 : W * t1],
+                out=h_codes[g, h][:, P * t0 : P * t1].bitcast(FP8X4),
+                scales=h_scales[g, h][:, P * t0 : P * t1],
+                in_=h_cols[g, h][:, W * t0 : W * t1],
             )
 
         e_side = [keep("e_side%d" % c, [P, 2, W, 4], BF16) for c in range(3)]
         e_codes = [keep("e_codes%d" % c, [P, 2, W], U32) for c in range(3)]
         e_scales = [keep("e_scales%d" % c, [P, 2, W], U8) for c in range(3)]
 
-        def lay_err(engine, h, c, lo=0, hi=W):
-            side_by_side(engine, e_side[c][:, h, lo:hi, :], e_raw[(h, c)][:, :, lo:hi])
+        def lay_err(copy, h, c):
+            side_by_side(copy, e_side[c][:, h, :, :], e_rows[h, c][:])
 
         def quant_err(c, h0, h1):
             nc.vector.quantize_mx(
@@ -166,268 +161,286 @@ def tile_gptq_damped_gram_error_k5_kernel(
                 in_=e_side[c][:, h0:h1, :, :].rearrange("p h n t -> p (h n t)"),
             )
 
-        def product_pass(u, t, h):
-            g, n0, w = u
-            c, o = divmod(n0, W)
+        def product_pass(unit, t, h):
+            g, first, width = UNITS[unit]
+            c, at = divmod(first, W)
             if h == 0:
-                take_bank(("prod", u, t))
-            bank = held[("prod", u, t)][1]
+                take_bank(("product", unit, t))
             nc.tensor.matmul_mx(
-                out=bank[:, :w],
-                lhsT=h_codes[(g, h)][:, P * t : P * (t + 1)].bitcast(FP8X4),
-                lhsT_scale=h_scales[(g, h)][:, P * t : P * (t + 1)],
-                rhs=e_codes[c][:, h, o : o + w].bitcast(FP8X4),
-                rhs_scale=e_scales[c][:, h, o : o + w],
+                out=bank_of(("product", unit, t))[:, :width],
+                lhsT=h_codes[g, h][:, P * t : P * (t + 1)].bitcast(FP8X4),
+                lhsT_scale=h_scales[g, h][:, P * t : P * (t + 1)],
+                rhs=e_codes[c][:, h, at : at + width].bitcast(FP8X4),
+                rhs_scale=e_scales[c][:, h, at : at + width],
                 start=(h == 0),
                 stop=(h == 1),
             )
 
-        def product(u, ts):
-            for t in ts:
+        def product(unit, *slices):
+            for t in slices:
                 for h in range(2):
-                    product_pass(u, t, h)
+                    product_pass(unit, t, h)
 
-        damped, y32, y16 = {}, {}, {}
+        y32 = [keep("y32_%d" % unit, [P, 4, UNITS[unit][2]], F32) for unit in range(len(UNITS))]
+        y16 = {}
 
-        def add_damping(u, t):
-            g, n0, w = u
-            c, o = divmod(n0, W)
-            if t == 0:
-                damped[u] = sb.tile([P, 4, w], F32, name="damped", tag="damped", bufs=3)
-                y32[u] = sb.tile([P, 4, w], F32, name="y32", tag="y32", bufs=4)
-            bank = give_bank(("prod", u, t))
+        def add_damping(unit, t):
+            g, first, width = UNITS[unit]
+            c, at = divmod(first, W)
+            bank = give_bank(("product", unit, t))
             nc.vector.scalar_tensor_tensor(
-                out=damped[u][:, t, :], in0=e_raw[(g, c)][:, t, o : o + w], scalar=damp_sb[:, g, t : t + 1],
-                in1=bank[:, :w], op0=MULT, op1=ADD,
+                out=y32[unit][:, t, :],
+                in0=e_rows[g, c][:, t, at : at + width],
+                scalar=damp_rows[:, g, t : t + 1],
+                in1=bank[:, :width],
+                op0=MULT,
+                op1=ADD,
             )
 
-        def pool_step(u, t, lo, hi):
-            g, n0, w = u
+        def store_y(unit, t0, t1):
+            g, first, width = UNITS[unit]
+            dst = out_0[W * g : W * (g + 1), first : first + width].rearrange("(p t) n -> p t n", t=4)
+            nc.sync.dma_start(out=dst[:, t0:t1, :], in_=y32[unit][:, t0:t1, :])
+
+        def step_on_gpsimd(unit, t):
+            first, width = UNITS[unit][1:]
             nc.gpsimd.tensor_tensor(
-                out=y32[u][:, t, lo:hi], in0=damped[u][:, t, lo:hi], in1=step_all[:, n0 + lo : n0 + hi], op=MULT
+                out=y32[unit][:, t, :], in0=y32[unit][:, t, :], in1=step_sbuf[:, first : first + width], op=MULT
             )
 
-        def vector_step(u, t, lo, hi):
-            g, n0, w = u
-            c, o = divmod(n0, W)
+        def step_on_vector(unit, t):
+            c, at = divmod(UNITS[unit][1], W)
             nc.vector.tensor_tensor(
-                out=y32[u][:, t, lo:hi].rearrange("q (p b e) -> q p b e", b=2, e=2),
-                in0=damped[u][:, t, lo:hi].rearrange("q (p b e) -> q p b e", b=2, e=2),
-                in1=step_psum[c][:, (o + lo) // 4 : (o + hi) // 4, :, :],
-                op=MULT,
+                out=y32[unit][:, t, :], in0=y32[unit][:, t, :], in1=step_psum[c][:, at : at + UNITS[unit][2]], op=MULT
             )
 
-        def store_y(u, t0, t1):
-            g, n0, w = u
-            nc.sync.dma_start(
-                out=out_0[W * g : W * (g + 1), n0 : n0 + w].rearrange("(p t) n -> p t n", t=4)[:, t0:t1, :],
-                in_=y32[u][:, t0:t1, :],
-            )
-
-        def round_y(engine, u, lo, hi):
-            if u not in y16:
-                y16[u] = sb.tile([P, u[2], 4], BF16, name="y16", tag="y16", bufs=3, align_bytes=64)
-            side_by_side(engine, y16[u][:, lo:hi, :], y32[u][:, :, lo:hi])
+        def round_y(copy, unit, lo, hi):
+            if unit not in y16:
+                y16[unit] = sb.tile([P, UNITS[unit][2], 4], BF16, name="y16", tag="y16", bufs=3, align_bytes=256)
+            side_by_side(copy, y16[unit][:, lo:hi, :], y32[unit][:, :, lo:hi])
 
         y_codes = [keep("y_codes%d" % g, [P, N], U32) for g in range(2)]
         y_scales = [keep("y_scales%d" % g, [P, N], U8) for g in range(2)]
         dst_words = out_1.rearrange("g p m t -> g p (m t)").bitcast(I32)
         dst_scales = out_2.bitcast(I32)
 
-        def quant_y(u):
-            g, n0, w = u
+        def quant_y(unit):
+            g, first, width = UNITS[unit]
+            cols = slice(first, first + width)
             nc.vector.quantize_mx(
-                out=y_codes[g][:, n0 : n0 + w].bitcast(FP8X4),
-                scales=y_scales[g][:, n0 : n0 + w],
-                in_=y16[u][:].rearrange("p n t -> p (n t)"),
+                out=y_codes[g][:, cols].bitcast(FP8X4),
+                scales=y_scales[g][:, cols],
+                in_=y16[unit][:].rearrange("p n t -> p (n t)"),
             )
-            nc.sync.dma_start(out=dst_words[g, :, n0 : n0 + w], in_=y_codes[g][:, n0 : n0 + w].bitcast(I32))
+            nc.sync.dma_start(out=dst_words[g, :, cols], in_=y_codes[g][:, cols].bitcast(I32))
 
-        def store_scales(g, lo, hi, queues):
-            for r in range(4):
-                queues[r].dma_start(
-                    out=dst_scales[g, r:16:4, lo // 4 : hi // 4], in_=y_scales[g][r:P:32, lo:hi].bitcast(I32)
-                )
+        def store_scales(g, queues):
+            for r, queue in enumerate(queues):
+                queue.dma_start(out=dst_scales[g, r:16:4, :], in_=y_scales[g][r:P:32, :].bitcast(I32))
+
+        on_scalar, on_vector = nc.scalar.copy, nc.vector.tensor_copy
 
         step_cols = keep("step_cols", [P, 3, 4], BF16)
-        damp_sb = keep("damp_sb", [P, 2, 4], BF16)
+        damp_rows = keep("damp_rows", [P, 2, 4], BF16)
         ident = keep("ident", [P, P], F32)
-        step_all = keep("step_all", [P, N], F32)
+        step_sbuf = keep("step_sbuf", [P, N], F32)
 
-        nc.gpsimd.dma_start(out=step_cols[:], in_=step.rearrange("(c p b) -> p c b", c=3, b=4))
+        nc.sync.dma_start(out=step_cols[:], in_=step.rearrange("(c p b) -> p c b", c=3, b=4))
         for half in range(2):
-            for op in (X, XW):
-                nc.vector.memset(planes[(op, half)][:].rearrange("p g w -> p (g w)").bitcast(I32), 0)
+            for op in (XW, X):
+                nc.vector.memset(fp4_scales[op, half][:].rearrange("p g w -> p (g w)").bitcast(I32), 0)
         make_identity(nc, ident[:])
-        nc.gpsimd.dma_start(out=damp_sb[:], in_=damp.rearrange("(g p t) -> p g t", g=2, t=4))
-        load_words(X, 0, 0, 1)
-        load_words(XW, 0, 0, 1)
-        load_scales(X, 0)
+        nc.gpsimd.dma_start(out=damp_rows[:], in_=damp.rearrange("(g p t) -> p g t", g=2, t=4))
+        load_words(XW, [0], [0, 1])
         load_scales(XW, 0)
-        load_words(X, 0, 1, 2)
-        load_words(XW, 0, 1, 2)
-        load_words(X, 0, 2, 4)
-        load_words(XW, 0, 2, 4)
+        load_words(X, [0, 1], [0])
+        load_scales(X, 0)
+        load_words(X, [0, 1], [1])
+        load_words(XW, [0], [2, 3])
+        load_words(X, [0, 1], [2, 3])
         load_err(0, 0)
         load_scales(X, 1)
-        load_words(X, 1, 0, 4)
-        load_prior(0, 0, 0, 4)
+        load_prior(0, [0, 1])
         load_err(1, 0)
-        load_prior(0, 1, 0, 2)
-        load_prior(0, 1, 2, 4)
+        load_prior(0, [2])
+        load_prior(0, [3])
+        load_words(XW, [1], [0, 1, 2, 3])
         load_scales(XW, 1)
-        load_words(XW, 1, 0, 4)
         load_err(0, 1)
         load_err(1, 1)
-        load_prior(1, 0, 0, 4)
+        load_prior(1, [0, 1])
         load_err(0, 2)
+        load_prior(1, [2, 3])
         load_err(1, 2)
-        load_prior(1, 1, 0, 4)
 
         step_pairs = step_cols[:].bitcast(F32)
-        step_banks = [ps.tile([P, W], F32, name="step_bank%d" % i, tag="step_bank%d" % i) for i in range(2)]
+        step_banks = [ps.tile([P, W], F32, name="step_bank%d" % n, tag="step_bank%d" % n) for n in range(2)]
         step_psum = []
         for c in range(3):
-            half_bank = step_banks[c // 2][:, 256 * (c % 2) : 256 * (c % 2 + 1)]
+            chunk = step_banks[c // 2][:, 2 * P * (c % 2) : 2 * P * (c % 2 + 1)]
             for b in range(2):
-                nc.tensor.transpose(
-                    half_bank[:, P * b : P * (b + 1)], step_pairs[:, c, b : b + 1].to_broadcast([P, P]), ident[:]
-                )
-            step_psum.append(half_bank.bitcast(BF16).rearrange("q (b p e) -> q p b e", b=2, e=2))
+                nc.tensor.transpose(chunk[:, b : 2 * P : 2], step_pairs[:, c, b : b + 1].to_broadcast([P, P]), ident[:])
+            step_psum.append(chunk.bitcast(BF16))
         for c in range(3):
-            nc.scalar.copy(
-                out=step_all[:, W * c : W * (c + 1)].rearrange("q (p b e) -> q p b e", b=2, e=2), in_=step_psum[c]
+            nc.scalar.copy(out=step_sbuf[:, W * c : W * (c + 1)], in_=step_psum[c])
+
+        take_bank("warm")
+        for a in range(3):
+            nc.tensor.matmul_mx(
+                out=bank_of("warm")[:],
+                lhsT=fp4_words[XW, 0, 0][:, 2 * P * a : 2 * P * (a + 1)].bitcast(FP4X4),
+                lhsT_scale=fp4_scales[XW, 0][:, 0, P * a : P * (a + 1)],
+                rhs=fp4_words[XW, 0, 0].bitcast(FP4X4),
+                rhs_scale=fp4_scales[XW, 0][:, 0, :],
+                start=True,
+                stop=True,
             )
+        give_bank("warm")
 
         for tg in range(4):
             for a in range(4):
                 gram_pass(0, 0, a, tg)
-        lay_err("V", 0, 0)
+        lay_err(on_vector, 0, 0)
         quant_err(0, 0, 1)
-        lay_err("S", 1, 0)
+        lay_err(on_scalar, 1, 0)
         gram(0, 1, 0)
         gram(0, 1, 1)
-        for a in range(4):
-            add_prior(0, 0, a)
+        add_prior(0, 0, 0)
+        add_prior(0, 0, 1)
         gram(0, 1, 2)
         gram(0, 1, 3)
-        add_prior(0, 1, 0)
-        add_prior(0, 1, 1)
-        turn(0, 0, 0)
-        turn(0, 0, 1)
-        turn(0, 1, 0)
-        add_prior(0, 1, 2)
-        add_prior(0, 1, 3)
-        turn(0, 1, 1)
-        spill("S", 0, 0, 0)
-        spill("S", 0, 0, 1)
-        spill("S", 0, 1, 0)
-        spill("S", 0, 1, 1)
-        gram(1, 0, 0)
-        gram(1, 0, 1)
+        for h, a in ((1, 0), (1, 1), (0, 2), (1, 2), (0, 3), (1, 3)):
+            add_prior(0, h, a)
         quant_err(0, 1, 2)
-        quant_h(0, 0, 0, 4)
+        for pair in range(2):
+            for h in range(2):
+                turn(0, h, pair)
+        spill(on_scalar, 0, 0, 0)
+        spill(on_scalar, 0, 1, 0)
+        spill(on_vector, 0, 0, 1)
+        spill(on_scalar, 0, 1, 1)
+        gram(1, 0, 0)
+        quant_h(0, 0, 0, 2)
         quant_h(0, 1, 0, 2)
+        quant_h(0, 0, 2, 4)
         quant_h(0, 1, 2, 4)
-        lay_err("S", 0, 1)
-        lay_err("S", 1, 1)
-        u = [(0, 0, W), (0, W, W), (0, 2 * W, W), (1, 0, W), (1, W, W), (1, 2 * W, 256), (1, 2 * W + 256, 128), (1, 2 * W + 384, 128)]
+        for c in (1, 2):
+            for h in range(2):
+                lay_err(on_scalar, h, c)
 
-        product(u[0], range(4))
-        add_damping(u[0], 0)
-        pool_step(u[0], 0, 0, W)
-        add_damping(u[0], 1)
-        pool_step(u[0], 1, 0, W)
-        add_damping(u[0], 2)
-        pool_step(u[0], 2, 0, 256)
-        add_damping(u[0], 3)
+        def gpsimd_slice(unit, t):
+            step_on_gpsimd(unit, t)
+            store_y(unit, t, t + 1)
+
+        def vector_slice(unit, t):
+            step_on_vector(unit, t)
+            store_y(unit, t, t + 1)
+
+        product_pass(0, 0, 0)
+        product_pass(0, 1, 0)
+        product_pass(0, 0, 1)
+        product_pass(0, 1, 1)
+        product(0, 2, 3)
+        gram(1, 0, 1)
+        for t in range(2):
+            add_damping(0, t)
+            gpsimd_slice(0, t)
+        add_damping(0, 2)
         gram(1, 0, 2)
         gram(1, 0, 3)
         add_prior(1, 0, 0)
-        vector_step(u[0], 3, 0, W)
-        vector_step(u[0], 2, 256, W)
+        vector_slice(0, 2)
         add_prior(1, 0, 1)
-        store_y(u[0], 0, 2)
-        store_y(u[0], 2, 4)
-        quant_err(1, 0, 2)
-        lay_err("S", 0, 2)
-        round_y("S", u[0], 0, W)
-        lay_err("S", 1, 2)
-        product(u[1], range(4))
-        add_prior(1, 0, 2)
-        add_prior(1, 0, 3)
-        add_damping(u[1], 0)
-        pool_step(u[1], 0, 0, W)
         gram(1, 1, 0)
-        add_damping(u[1], 1)
-        pool_step(u[1], 1, 0, W)
+        add_damping(0, 3)
+        quant_err(1, 0, 2)
+        gpsimd_slice(0, 3)
+
+        product(1, 0, 1, 2)
+        add_prior(1, 0, 2)
+        product(1, 3)
+        add_prior(1, 0, 3)
+        add_damping(1, 0)
+        quant_err(2, 0, 1)
+        gpsimd_slice(1, 0)
         turn(1, 0, 0)
-        add_damping(u[1], 2)
-        pool_step(u[1], 2, 0, 256)
+        add_damping(1, 1)
+        gpsimd_slice(1, 1)
         turn(1, 0, 1)
-        add_damping(u[1], 3)
-        spill("S", 1, 0, 0)
-        spill("S", 1, 0, 1)
+        add_damping(1, 2)
         gram(1, 1, 1)
-        vector_step(u[1], 2, 256, W)
-        vector_step(u[1], 3, 0, W)
-        store_y(u[1], 0, 2)
-        store_y(u[1], 2, 4)
-        round_y("S", u[1], 0, W)
         add_prior(1, 1, 0)
-        quant_err(2, 0, 2)
-        quant_y(u[0])
+        vector_slice(1, 2)
+        spill(on_scalar, 1, 0, 0)
+        spill(on_scalar, 1, 0, 1)
+        round_y(on_scalar, 0, 0, W)
         gram(1, 1, 2)
-        product(u[2], [0, 1])
+        add_damping(1, 3)
+        quant_err(2, 1, 2)
+        gpsimd_slice(1, 3)
         gram(1, 1, 3)
+
         add_prior(1, 1, 1)
         add_prior(1, 1, 2)
-        product(u[2], [2, 3])
-        add_damping(u[2], 0)
+        product(2, 0, 1)
         quant_h(1, 0, 0, 4)
-        pool_step(u[2], 0, 0, W)
         add_prior(1, 1, 3)
         turn(1, 1, 0)
-        add_damping(u[2], 1)
-        pool_step(u[2], 1, 0, W)
         turn(1, 1, 1)
-        spill("S", 1, 1, 0)
-        spill("S", 1, 1, 1)
-        add_damping(u[2], 2)
-        add_damping(u[2], 3)
-        for t in range(4):
-            product_pass(u[3], t, 0)
-        vector_step(u[2], 2, 0, W)
+        product(2, 2, 3)
+        spill(on_scalar, 1, 1, 0)
+        spill(on_scalar, 1, 1, 1)
+        round_y(on_scalar, 1, 0, W)
+        add_damping(2, 0)
+        quant_y(0)
+        gpsimd_slice(2, 0)
+        add_damping(2, 1)
+        add_damping(2, 2)
         quant_h(1, 1, 0, 4)
+        gpsimd_slice(2, 2)
+        add_damping(2, 3)
+        vector_slice(2, 1)
+        product(3, 0, 1, 2, 3)
+        vector_slice(2, 3)
+        round_y(on_scalar, 2, 0, W)
+
+        for unit in (3, 4):
+            for t in range(4):
+                add_damping(unit, t)
+                if t == 0:
+                    quant_y(unit - 2)
+                    if unit == 4:
+                        store_scales(0, [nc.sync] * 4)
+                if t < 2:
+                    gpsimd_slice(unit, t)
+                product(unit + 1, t)
+            vector_slice(unit, 2)
+            vector_slice(unit, 3)
+            round_y(on_scalar, unit, 0, W)
+
         for t in range(4):
-            product_pass(u[3], t, 1)
-        vector_step(u[2], 3, 0, W)
-        store_y(u[2], 0, 2)
-        store_y(u[2], 2, 4)
-        round_y("S", u[2], 0, W)
-        quant_y(u[1])
-        share = {3: 1024, 4: 1024, 5: 512, 6: 128, 7: 0}
-        for i in range(3, 8):
-            w = u[i][2]
-            for t in range(4):
-                add_damping(u[i], t)
-                if t == 0 and i > 3:
-                    quant_y(u[i - 2])
-                n = min(max(share[i] - t * w, 0), w)
-                if n > 0:
-                    pool_step(u[i], t, 0, n)
-                if i + 1 < 8:
-                    product(u[i + 1], [t])
-            for t in range(4):
-                n = min(max(share[i] - t * w, 0), w)
-                if n < w:
-                    vector_step(u[i], t, n, w)
-            store_y(u[i], 0, 2)
-            store_y(u[i], 2, 4)
-            round_y("S", u[i], 0, w)
-            if i == 4:
-                store_scales(0, 0, N, [nc.sync] * 4)
-        quant_y(u[6])
-        store_scales(1, 0, N - 128, [nc.sync] * 4)
-        quant_y(u[7])
-        store_scales(1, N - 128, N, [nc.scalar, nc.scalar, nc.sync, nc.sync])
+            add_damping(5, t)
+            if t == 0:
+                quant_y(3)
+            if t != 2:
+                step_on_gpsimd(5, t)
+            if t == 1:
+                store_y(5, 0, 2)
+            product(6, t)
+        step_on_vector(5, 2)
+        store_y(5, 2, 4)
+        round_y(on_scalar, 5, 0, 256)
+        for t in range(4):
+            add_damping(6, t)
+        step_on_gpsimd(6, 3)
+        quant_y(4)
+        step_on_vector(6, 0)
+        step_on_vector(6, 1)
+        store_y(6, 0, 2)
+        step_on_vector(6, 2)
+        store_y(6, 2, 4)
+        quant_y(5)
+        round_y(on_scalar, 6, 0, P)
+        round_y(on_vector, 6, P, 2 * P)
+        quant_y(6)
+        store_scales(1, [nc.scalar, nc.scalar, nc.sync, nc.sync])

@@ -66,10 +66,10 @@ def tile_gptq_damped_gram_error_k5_kernel(
                 for m, half in enumerate(halves):
                     fp4_words[op, half, tg] = tile[:, n, 2 * W * m : 2 * W * (m + 1)]
 
-        def load_scales(op, half):
+        def load_scales(queue, op, half):
             for r in range(4):
                 src = src_scales[op][:, r:16:4, P * half : P * (half + 1)]
-                nc.sync.dma_start(
+                queue.dma_start(
                     out=fp4_scales[op, half][r:P:32, :, :].bitcast(I32), in_=src.rearrange("g q w -> q g w")
                 )
 
@@ -112,8 +112,8 @@ def tile_gptq_damped_gram_error_k5_kernel(
             h_rows[g, h, a] = keep("h_rows%d_%d" % (h, a), [P, W], BF16)
             nc.vector.tensor_tensor(
                 out=h_rows[g, h, a][:].rearrange("r (u p e) -> r u p e", u=2, e=2),
-                in0=bank[:].rearrange("r (p u e) -> r u p e", u=2, e=2),
-                in1=p_rows[g, a][:, W * h : W * (h + 1)].rearrange("r (p u e) -> r u p e", u=2, e=2),
+                in0=p_rows[g, a][:, W * h : W * (h + 1)].rearrange("r (p u e) -> r u p e", u=2, e=2),
+                in1=bank[:].rearrange("r (p u e) -> r u p e", u=2, e=2),
                 op=ADD,
             )
 
@@ -202,17 +202,16 @@ def tile_gptq_damped_gram_error_k5_kernel(
             dst = out_0[W * g : W * (g + 1), first : first + width].rearrange("(p t) n -> p t n", t=4)
             nc.sync.dma_start(out=dst[:, t0:t1, :], in_=y32[unit][:, t0:t1, :])
 
-        def step_on_gpsimd(unit, t):
-            first, width = UNITS[unit][1:]
-            nc.gpsimd.tensor_tensor(
-                out=y32[unit][:, t, :], in0=y32[unit][:, t, :], in1=step_sbuf[:, first : first + width], op=MULT
-            )
+        def step_on_gpsimd(unit, t, upto):
+            first = UNITS[unit][1]
+            cols = y32[unit][:, t, :upto]
+            nc.gpsimd.tensor_tensor(out=cols, in0=cols, in1=step_sbuf[:, first : first + upto], op=MULT)
 
-        def step_on_vector(unit, t):
-            c, at = divmod(UNITS[unit][1], W)
-            nc.vector.tensor_tensor(
-                out=y32[unit][:, t, :], in0=y32[unit][:, t, :], in1=step_psum[c][:, at : at + UNITS[unit][2]], op=MULT
-            )
+        def step_on_vector(unit, t, start):
+            first, width = UNITS[unit][1:]
+            c, at = divmod(first, W)
+            cols = y32[unit][:, t, start:]
+            nc.vector.tensor_tensor(out=cols, in0=cols, in1=step_psum[c][:, at + start : at + width], op=MULT)
 
         def round_y(copy, unit, lo, hi):
             if unit not in y16:
@@ -246,26 +245,25 @@ def tile_gptq_damped_gram_error_k5_kernel(
         step_sbuf = keep("step_sbuf", [P, N], F32)
 
         nc.sync.dma_start(out=step_cols[:], in_=step.rearrange("(c p b) -> p c b", c=3, b=4))
-        for half in range(2):
-            for op in (XW, X):
-                nc.vector.memset(fp4_scales[op, half][:].rearrange("p g w -> p (g w)").bitcast(I32), 0)
+        for op, half in ((XW, 0), (X, 0), (X, 1), (XW, 1)):
+            nc.vector.memset(fp4_scales[op, half][:].rearrange("p g w -> p (g w)").bitcast(I32), 0)
         make_identity(nc, ident[:])
-        nc.gpsimd.dma_start(out=damp_rows[:], in_=damp.rearrange("(g p t) -> p g t", g=2, t=4))
+        load_scales(nc.gpsimd, X, 1)
+        load_scales(nc.gpsimd, XW, 1)
         load_words(XW, [0], [0, 1])
-        load_scales(XW, 0)
+        load_scales(nc.sync, XW, 0)
         load_words(X, [0, 1], [0])
-        load_scales(X, 0)
+        load_scales(nc.sync, X, 0)
         load_words(X, [0, 1], [1])
         load_words(XW, [0], [2, 3])
         load_words(X, [0, 1], [2, 3])
         load_err(0, 0)
-        load_scales(X, 1)
         load_prior(0, [0, 1])
         load_err(1, 0)
         load_prior(0, [2])
         load_prior(0, [3])
+        nc.sync.dma_start(out=damp_rows[:], in_=damp.rearrange("(g p t) -> p g t", g=2, t=4))
         load_words(XW, [1], [0, 1, 2, 3])
-        load_scales(XW, 1)
         load_err(0, 1)
         load_err(1, 1)
         load_prior(1, [0, 1])
@@ -301,12 +299,12 @@ def tile_gptq_damped_gram_error_k5_kernel(
             for a in range(4):
                 gram_pass(0, 0, a, tg)
         lay_err(on_vector, 0, 0)
-        quant_err(0, 0, 1)
         lay_err(on_scalar, 1, 0)
         gram(0, 1, 0)
         gram(0, 1, 1)
         add_prior(0, 0, 0)
         add_prior(0, 0, 1)
+        quant_err(0, 0, 1)
         gram(0, 1, 2)
         gram(0, 1, 3)
         for h, a in ((1, 0), (1, 1), (0, 2), (1, 2), (0, 3), (1, 3)):
@@ -329,11 +327,11 @@ def tile_gptq_damped_gram_error_k5_kernel(
                 lay_err(on_scalar, h, c)
 
         def gpsimd_slice(unit, t):
-            step_on_gpsimd(unit, t)
+            step_on_gpsimd(unit, t, W)
             store_y(unit, t, t + 1)
 
-        def vector_slice(unit, t):
-            step_on_vector(unit, t)
+        def vector_slice(unit, t, start=0):
+            step_on_vector(unit, t, start)
             store_y(unit, t, t + 1)
 
         product_pass(0, 0, 0)
@@ -349,12 +347,13 @@ def tile_gptq_damped_gram_error_k5_kernel(
         gram(1, 0, 2)
         gram(1, 0, 3)
         add_prior(1, 0, 0)
-        vector_slice(0, 2)
         add_prior(1, 0, 1)
         gram(1, 1, 0)
         add_damping(0, 3)
         quant_err(1, 0, 2)
         gpsimd_slice(0, 3)
+        step_on_gpsimd(0, 2, W // 2)
+        vector_slice(0, 2, W // 2)
 
         product(1, 0, 1, 2)
         add_prior(1, 0, 2)
@@ -370,7 +369,7 @@ def tile_gptq_damped_gram_error_k5_kernel(
         add_damping(1, 2)
         gram(1, 1, 1)
         add_prior(1, 1, 0)
-        vector_slice(1, 2)
+        gpsimd_slice(1, 2)
         spill(on_scalar, 1, 0, 0)
         spill(on_scalar, 1, 0, 1)
         round_y(on_scalar, 0, 0, W)
@@ -401,7 +400,8 @@ def tile_gptq_damped_gram_error_k5_kernel(
         add_damping(2, 3)
         vector_slice(2, 1)
         product(3, 0, 1, 2, 3)
-        vector_slice(2, 3)
+        step_on_gpsimd(2, 3, W // 2)
+        vector_slice(2, 3, W // 2)
         round_y(on_scalar, 2, 0, W)
 
         for unit in (3, 4):
@@ -413,8 +413,10 @@ def tile_gptq_damped_gram_error_k5_kernel(
                         store_scales(0, [nc.sync] * 4)
                 if t < 2:
                     gpsimd_slice(unit, t)
+                if t == 2:
+                    step_on_gpsimd(unit, t, W // 4)
                 product(unit + 1, t)
-            vector_slice(unit, 2)
+            vector_slice(unit, 2, W // 4)
             vector_slice(unit, 3)
             round_y(on_scalar, unit, 0, W)
 
@@ -423,21 +425,21 @@ def tile_gptq_damped_gram_error_k5_kernel(
             if t == 0:
                 quant_y(3)
             if t != 2:
-                step_on_gpsimd(5, t)
+                step_on_gpsimd(5, t, 256)
             if t == 1:
                 store_y(5, 0, 2)
             product(6, t)
-        step_on_vector(5, 2)
+        step_on_vector(5, 2, 0)
         store_y(5, 2, 4)
         round_y(on_scalar, 5, 0, 256)
         for t in range(4):
             add_damping(6, t)
-        step_on_gpsimd(6, 3)
+        step_on_gpsimd(6, 3, 256)
         quant_y(4)
-        step_on_vector(6, 0)
-        step_on_vector(6, 1)
+        step_on_vector(6, 0, 0)
+        step_on_vector(6, 1, 0)
         store_y(6, 0, 2)
-        step_on_vector(6, 2)
+        step_on_vector(6, 2, 0)
         store_y(6, 2, 4)
         quant_y(5)
         round_y(on_scalar, 6, 0, P)

@@ -282,19 +282,6 @@ def tile_gptq_damped_gram_error_k5_kernel(
         for c in range(3):
             nc.scalar.copy(out=step_sbuf[:, W * c : W * (c + 1)], in_=step_psum[c])
 
-        take_bank("warm")
-        for a in range(3):
-            nc.tensor.matmul_mx(
-                out=bank_of("warm")[:],
-                lhsT=fp4_words[XW, 0, 0][:, 2 * P * a : 2 * P * (a + 1)].bitcast(FP4X4),
-                lhsT_scale=fp4_scales[XW, 0][:, 0, P * a : P * (a + 1)],
-                rhs=fp4_words[XW, 0, 0].bitcast(FP4X4),
-                rhs_scale=fp4_scales[XW, 0][:, 0, :],
-                start=True,
-                stop=True,
-            )
-        give_bank("warm")
-
         for tg in range(4):
             for a in range(4):
                 gram_pass(0, 0, a, tg)

from contextlib import ExitStack

import concourse.mybir as mybir
from concourse.masks import make_identity

T, K, N = 2048, 1024, 1536
FLOPS = 2 * T * K * K + 2 * K * K * N

F32 = mybir.dt.float32
BF16 = mybir.dt.bfloat16
I32 = mybir.dt.int32
U32 = mybir.dt.uint32
U8 = mybir.dt.uint8
FP8X4 = mybir.dt.float8_e4m3fn_x4
FP4X4 = mybir.dt.float4_e2m1fn_x4
ADD = mybir.AluOpType.add
MULT = mybir.AluOpType.mult

P = 128
W = 512
XW, X = 0, 1
WORK_BANKS = 6
UNITS = [(0, 0, W), (0, W, W), (0, 2 * W, W), (1, 0, W), (1, W, W), (1, 2 * W, 256), (1, 2 * W + 256, 256)]


def tile_gptq_damped_gram_error_k5_kernel(
    tc, xw_words, xw_scales, x_words, x_scales, prior, err, damp, step, out_0, out_1, out_2
):
    nc = tc.nc
    with ExitStack() as ctx:
        sb = ctx.enter_context(tc.tile_pool(name="sb", bufs=1))
        ps = ctx.enter_context(tc.psum_pool(name="ps", bufs=1))
        ctx.enter_context(tc.manual_schedule())

        def keep(name, shape, dtype):
            return sb.tile(shape, dtype, name=name, align_bytes=256)

        free_banks = list(range(WORK_BANKS))
        held = {}

        def take_bank(key):
            b = free_banks.pop(0)
            held[key] = (b, ps.tile([P, W], F32, name="bank%d" % b, tag="bank%d" % b))

        def bank_of(key):
            return held[key][1]

        def give_bank(key):
            b, bank = held.pop(key)
            free_banks.append(b)
            return bank

        src_words = [xw_words.bitcast(I32), x_words.bitcast(I32)]
        src_scales = [xw_scales.bitcast(I32), x_scales.bitcast(I32)]
        fp4_words = {}
        fp4_scales = {
            (op, half): keep("fp4_scales%d_%d" % (op, half), [P, 4, W], U8) for op in (XW, X) for half in range(2)
        }
        e_rows, p_rows = {}, {}

        def load_words(op, halves, tgs):
            tile = keep("fp4_words%d_%d_%d" % (op, halves[0], tgs[0]), [P, len(tgs), 2 * W * len(halves)], U8)
            src = src_words[op][tgs[0] : tgs[-1] + 1, :, 256 * halves[0] : 256 * (halves[-1] + 1)]
            nc.sync.dma_start(out=tile[:].bitcast(I32), in_=src.rearrange("g p w -> p g w"))
            for n, tg in enumerate(tgs):
                for m, half in enumerate(halves):
                    fp4_words[op, half, tg] = tile[:, n, 2 * W * m : 2 * W * (m + 1)]

        def load_scales(queue, op, half):
            for r in range(4):
                src = src_scales[op][:, r:16:4, P * half : P * (half + 1)]
                queue.dma_start(
                    out=fp4_scales[op, half][r:P:32, :, :].bitcast(I32), in_=src.rearrange("g q w -> q g w")
                )

        def load_err(h, c):
            e_rows[h, c] = keep("e_rows%d_%d" % (h, c), [P, 4, W], BF16)
            src = err[W * h : W * (h + 1), W * c : W * (c + 1)]
            nc.sync.dma_start(out=e_rows[h, c][:], in_=src.rearrange("(p t) n -> p t n", t=4))

        def load_prior(g, tiles):
            tile = keep("p_rows%d_%d" % (g, tiles[0]), [P, len(tiles), K], BF16)
            src = prior[W * g + P * tiles[0] : W * g + P * (tiles[-1] + 1), :]
            nc.sync.dma_start(out=tile[:], in_=src.rearrange("(a r) j -> r a j", r=P))
            for n, a in enumerate(tiles):
                p_rows[g, a] = tile[:, n, :]

        def side_by_side(copy, out, in_):
            copy(out=out.rearrange("p (c i) t -> p c t i", i=4), in_=in_.rearrange("p t (c i) -> p c t i", i=4))

        def gram_pass(g, h, a, tg):
            if tg == 0:
                take_bank(("gram", g, h, a))
            nc.tensor.matmul_mx(
                out=bank_of(("gram", g, h, a))[:],
                lhsT=fp4_words[XW, g, tg][:, 2 * P * a : 2 * P * (a + 1)].bitcast(FP4X4),
                lhsT_scale=fp4_scales[XW, g][:, tg, P * a : P * (a + 1)],
                rhs=fp4_words[X, h, tg].bitcast(FP4X4),
                rhs_scale=fp4_scales[X, h][:, tg, :],
                start=(tg == 0),
                stop=(tg == 3),
            )

        def gram(g, h, a):
            for tg in range(4):
                gram_pass(g, h, a, tg)

        h_rows = {}

        def add_prior(g, h, a):
            bank = give_bank(("gram", g, h, a))
            h_rows[g, h, a] = keep("h_rows%d_%d" % (h, a), [P, W], BF16)
            nc.vector.tensor_tensor(
                out=h_rows[g, h, a][:].rearrange("r (u p e) -> r u p e", u=2, e=2),
                in0=p_rows[g, a][:, W * h : W * (h + 1)].rearrange("r (p u e) -> r u p e", u=2, e=2),
                in1=bank[:].rearrange("r (p u e) -> r u p e", u=2, e=2),
                op=ADD,
            )

        def turn(g, h, pair):
            take_bank(("turn", g, h, pair))
            for n in range(2):
                pairs = h_rows[g, h, 2 * pair + n][:].bitcast(F32)
                for u in range(2):
                    at = 2 * P * u + P * n
                    nc.tensor.transpose(
                        bank_of(("turn", g, h, pair))[:, at : at + P], pairs[:, P * u : P * (u + 1)], ident[:]
                    )

        halves_of_h = [(g, h) for g in range(2) for h in range(2)]
        h_cols = {key: keep("h_cols%d_%d" % key, [P, 4 * W], BF16) for key in halves_of_h}
        h_codes = {key: keep("h_codes%d_%d" % key, [P, W], U32) for key in halves_of_h}
        h_scales = {key: keep("h_scales%d_%d" % key, [P, W], U8) for key in halves_of_h}

        def spill(copy, g, h, pair):
            bank = give_bank(("turn", g, h, pair))
            dst = h_cols[g, h][:].bitcast(F32).rearrange("p (t m u) -> p t m u", t=4, u=2)
            copy(
                out=dst[:, :, 64 * pair : 64 * (pair + 1), :],
                in_=bank[:].rearrange("p (u m t) -> p t m u", u=2, t=4),
            )

        def quant_h(g, h, t0, t1):
            nc.vector.quantize_mx(
                out=h_codes[g, h][:, P * t0 : P * t1].bitcast(FP8X4),
                scales=h_scales[g, h][:, P * t0 : P * t1],
                in_=h_cols[g, h][:, W * t0 : W * t1],
            )

        e_side = [keep("e_side%d" % c, [P, 2, W, 4], BF16) for c in range(3)]
        e_codes = [keep("e_codes%d" % c, [P, 2, W], U32) for c in range(3)]
        e_scales = [keep("e_scales%d" % c, [P, 2, W], U8) for c in range(3)]

        def lay_err(copy, h, c):
            side_by_side(copy, e_side[c][:, h, :, :], e_rows[h, c][:])

        def quant_err(c, h0, h1):
            nc.vector.quantize_mx(
                out=e_codes[c][:, h0:h1, :].rearrange("p h n -> p (h n)").bitcast(FP8X4),
                scales=e_scales[c][:, h0:h1, :].rearrange("p h n -> p (h n)"),
                in_=e_side[c][:, h0:h1, :, :].rearrange("p h n t -> p (h n t)"),
            )

        def product_pass(unit, t, h):
            g, first, width = UNITS[unit]
            c, at = divmod(first, W)
            if h == 0:
                take_bank(("product", unit, t))
            nc.tensor.matmul_mx(
                out=bank_of(("product", unit, t))[:, :width],
                lhsT=h_codes[g, h][:, P * t : P * (t + 1)].bitcast(FP8X4),
                lhsT_scale=h_scales[g, h][:, P * t : P * (t + 1)],
                rhs=e_codes[c][:, h, at : at + width].bitcast(FP8X4),
                rhs_scale=e_scales[c][:, h, at : at + width],
                start=(h == 0),
                stop=(h == 1),
            )

        def product(unit, *slices):
            for t in slices:
                for h in range(2):
                    product_pass(unit, t, h)

        y32 = [keep("y32_%d" % unit, [P, 4, UNITS[unit][2]], F32) for unit in range(len(UNITS))]
        y16 = {}

        def add_damping(unit, t):
            g, first, width = UNITS[unit]
            c, at = divmod(first, W)
            bank = give_bank(("product", unit, t))
            nc.vector.scalar_tensor_tensor(
                out=y32[unit][:, t, :],
                in0=e_rows[g, c][:, t, at : at + width],
                scalar=damp_rows[:, g, t : t + 1],
                in1=bank[:, :width],
                op0=MULT,
                op1=ADD,
            )

        def store_y(unit, t0, t1):
            g, first, width = UNITS[unit]
            dst = out_0[W * g : W * (g + 1), first : first + width].rearrange("(p t) n -> p t n", t=4)
            nc.sync.dma_start(out=dst[:, t0:t1, :], in_=y32[unit][:, t0:t1, :])

        def step_on_gpsimd(unit, t, upto):
            first = UNITS[unit][1]
            cols = y32[unit][:, t, :upto]
            nc.gpsimd.tensor_tensor(out=cols, in0=cols, in1=step_sbuf[:, first : first + upto], op=MULT)

        def step_on_vector(unit, t, start):
            first, width = UNITS[unit][1:]
            c, at = divmod(first, W)
            cols = y32[unit][:, t, start:]
            nc.vector.tensor_tensor(out=cols, in0=cols, in1=step_psum[c][:, at + start : at + width], op=MULT)

        def round_y(copy, unit, lo, hi):
            if unit not in y16:
                y16[unit] = sb.tile([P, UNITS[unit][2], 4], BF16, name="y16", tag="y16", bufs=3, align_bytes=256)
            side_by_side(copy, y16[unit][:, lo:hi, :], y32[unit][:, :, lo:hi])

        y_codes = [keep("y_codes%d" % g, [P, N], U32) for g in range(2)]
        y_scales = [keep("y_scales%d" % g, [P, N], U8) for g in range(2)]
        dst_words = out_1.rearrange("g p m t -> g p (m t)").bitcast(I32)
        dst_scales = out_2.bitcast(I32)

        def quant_y(unit):
            g, first, width = UNITS[unit]
            cols = slice(first, first + width)
            nc.vector.quantize_mx(
                out=y_codes[g][:, cols].bitcast(FP8X4),
                scales=y_scales[g][:, cols],
                in_=y16[unit][:].rearrange("p n t -> p (n t)"),
            )
            nc.sync.dma_start(out=dst_words[g, :, cols], in_=y_codes[g][:, cols].bitcast(I32))

        def store_scales(g, queues):
            for r, queue in enumerate(queues):
                queue.dma_start(out=dst_scales[g, r:16:4, :], in_=y_scales[g][r:P:32, :].bitcast(I32))

        on_scalar, on_vector = nc.scalar.copy, nc.vector.tensor_copy

        step_cols = keep("step_cols", [P, 3, 4], BF16)
        damp_rows = keep("damp_rows", [P, 2, 4], BF16)
        ident = keep("ident", [P, P], F32)
        step_sbuf = keep("step_sbuf", [P, N], F32)

        nc.sync.dma_start(out=step_cols[:], in_=step.rearrange("(c p b) -> p c b", c=3, b=4))
        for op, half in ((XW, 0), (X, 0), (X, 1), (XW, 1)):
            nc.vector.memset(fp4_scales[op, half][:].rearrange("p g w -> p (g w)").bitcast(I32), 0)
        make_identity(nc, ident[:])
        load_scales(nc.gpsimd, X, 1)
        load_scales(nc.gpsimd, XW, 1)
        load_words(XW, [0], [0, 1])
        load_scales(nc.sync, XW, 0)
        load_words(X, [0, 1], [0])
        load_scales(nc.sync, X, 0)
        load_words(X, [0, 1], [1])
        load_words(XW, [0], [2, 3])
        load_words(X, [0, 1], [2, 3])
        load_err(0, 0)
        load_prior(0, [0, 1])
        load_err(1, 0)
        load_prior(0, [2])
        load_prior(0, [3])
        nc.sync.dma_start(out=damp_rows[:], in_=damp.rearrange("(g p t) -> p g t", g=2, t=4))
        load_words(XW, [1], [0, 1, 2, 3])
        load_err(0, 1)
        load_err(1, 1)
        load_prior(1, [0, 1])
        load_err(0, 2)
        load_prior(1, [2, 3])
        load_err(1, 2)

        step_pairs = step_cols[:].bitcast(F32)
        step_banks = [ps.tile([P, W], F32, name="step_bank%d" % n, tag="step_bank%d" % n) for n in range(2)]
        step_psum = []
        for c in range(3):
            chunk = step_banks[c // 2][:, 2 * P * (c % 2) : 2 * P * (c % 2 + 1)]
            for b in range(2):
                nc.tensor.transpose(chunk[:, b : 2 * P : 2], step_pairs[:, c, b : b + 1].to_broadcast([P, P]), ident[:])
            step_psum.append(chunk.bitcast(BF16))
        for c in range(3):
            nc.scalar.copy(out=step_sbuf[:, W * c : W * (c + 1)], in_=step_psum[c])

        for tg in range(4):
            for a in range(4):
                gram_pass(0, 0, a, tg)
        lay_err(on_vector, 0, 0)
        lay_err(on_scalar, 1, 0)
        gram(0, 1, 0)
        gram(0, 1, 1)
        add_prior(0, 0, 0)
        add_prior(0, 0, 1)
        quant_err(0, 0, 1)
        gram(0, 1, 2)
        gram(0, 1, 3)
        for h, a in ((1, 0), (1, 1), (0, 2), (1, 2), (0, 3), (1, 3)):
            add_prior(0, h, a)
        quant_err(0, 1, 2)
        for pair in range(2):
            for h in range(2):
                turn(0, h, pair)
        spill(on_scalar, 0, 0, 0)
        spill(on_scalar, 0, 1, 0)
        spill(on_vector, 0, 0, 1)
        spill(on_scalar, 0, 1, 1)
        gram(1, 0, 0)
        quant_h(0, 0, 0, 2)
        quant_h(0, 1, 0, 2)
        quant_h(0, 0, 2, 4)
        quant_h(0, 1, 2, 4)
        for c in (1, 2):
            for h in range(2):
                lay_err(on_scalar, h, c)

        def gpsimd_slice(unit, t):
            step_on_gpsimd(unit, t, W)
            store_y(unit, t, t + 1)

        def vector_slice(unit, t, start=0):
            step_on_vector(unit, t, start)
            store_y(unit, t, t + 1)

        product_pass(0, 0, 0)
        product_pass(0, 1, 0)
        product_pass(0, 0, 1)
        product_pass(0, 1, 1)
        product(0, 2, 3)
        gram(1, 0, 1)
        for t in range(2):
            add_damping(0, t)
            gpsimd_slice(0, t)
        add_damping(0, 2)
        gram(1, 0, 2)
        gram(1, 0, 3)
        add_prior(1, 0, 0)
        add_prior(1, 0, 1)
        gram(1, 1, 0)
        add_damping(0, 3)
        quant_err(1, 0, 2)
        gpsimd_slice(0, 3)
        step_on_gpsimd(0, 2, W // 2)
        vector_slice(0, 2, W // 2)

        product(1, 0, 1, 2)
        add_prior(1, 0, 2)
        product(1, 3)
        add_prior(1, 0, 3)
        add_damping(1, 0)
        quant_err(2, 0, 1)
        gpsimd_slice(1, 0)
        turn(1, 0, 0)
        add_damping(1, 1)
        gpsimd_slice(1, 1)
        turn(1, 0, 1)
        add_damping(1, 2)
        gram(1, 1, 1)
        add_prior(1, 1, 0)
        gpsimd_slice(1, 2)
        spill(on_scalar, 1, 0, 0)
        spill(on_scalar, 1, 0, 1)
        round_y(on_scalar, 0, 0, W)
        gram(1, 1, 2)
        add_damping(1, 3)
        quant_err(2, 1, 2)
        gpsimd_slice(1, 3)
        gram(1, 1, 3)

        add_prior(1, 1, 1)
        add_prior(1, 1, 2)
        product(2, 0, 1)
        quant_h(1, 0, 0, 4)
        add_prior(1, 1, 3)
        turn(1, 1, 0)
        turn(1, 1, 1)
        product(2, 2, 3)
        spill(on_scalar, 1, 1, 0)
        spill(on_scalar, 1, 1, 1)
        round_y(on_scalar, 1, 0, W)
        add_damping(2, 0)
        quant_y(0)
        gpsimd_slice(2, 0)
        add_damping(2, 1)
        add_damping(2, 2)
        quant_h(1, 1, 0, 4)
        gpsimd_slice(2, 2)
        add_damping(2, 3)
        vector_slice(2, 1)
        product(3, 0, 1, 2, 3)
        step_on_gpsimd(2, 3, W // 2)
        vector_slice(2, 3, W // 2)
        round_y(on_scalar, 2, 0, W)

        for unit in (3, 4):
            for t in range(4):
                add_damping(unit, t)
                if t == 0:
                    quant_y(unit - 2)
                    if unit == 4:
                        store_scales(0, [nc.sync] * 4)
                if t < 2:
                    gpsimd_slice(unit, t)
                if t == 2:
                    step_on_gpsimd(unit, t, W // 4)
                product(unit + 1, t)
            vector_slice(unit, 2, W // 4)
            vector_slice(unit, 3)
            round_y(on_scalar, unit, 0, W)

        for t in range(4):
            add_damping(5, t)
            if t == 0:
                quant_y(3)
            if t != 2:
                step_on_gpsimd(5, t, 256)
            if t == 1:
                store_y(5, 0, 2)
            product(6, t)
        step_on_vector(5, 2, 0)
        store_y(5, 2, 4)
        round_y(on_scalar, 5, 0, 256)
        for t in range(4):
            add_damping(6, t)
        step_on_gpsimd(6, 3, 256)
        quant_y(4)
        step_on_vector(6, 0, 0)
        step_on_vector(6, 1, 0)
        store_y(6, 0, 2)
        step_on_vector(6, 2, 0)
        store_y(6, 2, 4)
        quant_y(5)
        round_y(on_scalar, 6, 0, P)
        round_y(on_vector, 6, P, 2 * P)
        quant_y(6)
        store_scales(1, [nc.scalar, nc.scalar, nc.sync, nc.sync])
